import numpy as np
import ml_dtypes


def mxq(x, axis, fmt="e4m3"):
    dtype, down = {"e4m3": (ml_dtypes.float8_e4m3fn, 7), "e5m2": (ml_dtypes.float8_e5m2, 14)}[fmt]
    v = np.moveaxis(np.asarray(x, np.float32).astype(ml_dtypes.bfloat16).astype(np.float64), axis, -1)
    blocks = v.reshape(v.shape[:-1] + (-1, 32))
    amax = np.abs(blocks).max(-1, keepdims=True)
    byte = np.maximum(np.where(amax > 0, np.frexp(amax)[1] - 1 + 127, 0) - down, 1)
    scale = np.exp2(byte - 127.0)
    codes = (blocks / scale).astype(np.float32).astype(dtype).astype(np.float64)
    return np.moveaxis((codes * scale).reshape(v.shape), -1, axis)


WIDE = False


def mx_kscale(k):
    if not WIDE:
        return np.ones(k)
    levels = np.array([10, -10, 5, -5, 0])
    if k % 512:
        return np.exp2(np.random.permutation(np.resize(levels, k // 32))).repeat(32)
    a = np.empty((k // 512, 16))
    for p in range(k // 512):
        a[p, :8] = np.random.permutation(np.resize(levels, 8))
        for g in range(8):
            far = levels[np.abs(levels - a[p, g]) >= 10]
            a[p, g + 8] = far[np.random.randint(len(far))]
    return np.exp2(a.ravel()).repeat(32)


def f64(x):
    return np.asarray(x).astype(np.float64)


def striped(idx):
    return np.tile(idx.reshape(-1, 16).T, (8, 1)).astype(np.uint16)


def unstriped(offs):
    return offs[:16].T.reshape(-1).astype(np.int64)


E2M1 = np.array([0.0, 0.5, 1.0, 1.5, 2.0, 3.0, 4.0, 6.0, -0.0, -0.5, -1.0, -1.5, -2.0, -3.0, -4.0, -6.0])


def pack_weight(w, fmt):
    k, n = w.shape
    w = f64(np.asarray(w, np.float32).astype(ml_dtypes.bfloat16)).reshape(k // 32, 32, n)
    amax = np.abs(w).max(1)
    if fmt == "e4m3":
        byte = np.frexp(amax)[1] - 1 + 127 - 7
    else:
        mant, ex = np.frexp(amax / 6.0)
        byte = np.where(mant > 0.5, ex, ex - 1) + 127
    byte = np.clip(np.where(amax > 0, byte, 1), 1, 254)
    scaled = (w * np.exp2(127.0 - byte)[:, None, :]).reshape(k, n).astype(np.float32)
    by_word = np.ascontiguousarray(scaled.reshape(k // 512, 128, 4, n).transpose(0, 1, 3, 2))
    if fmt == "e4m3":
        words = by_word.astype(ml_dtypes.float8_e4m3fn).view(np.uint8)
    else:
        c = by_word.astype(ml_dtypes.float4_e2m1fn).view(np.uint8) & 0xF
        words = (c[..., 0::2] | (c[..., 1::2] << 4)).reshape(k // 512, 128, 2 * n)
    return np.ascontiguousarray(words), np.ascontiguousarray(byte.astype(np.uint8).reshape(k // 512, 16, n))


def unpack_weight(words, scales, fmt):
    g, _, n = scales.shape
    words = np.ascontiguousarray(words).reshape(g, 128, n, -1)
    if fmt == "e4m3":
        vals = words.view(ml_dtypes.float8_e4m3fn).astype(np.float64)
    else:
        nib = np.empty((g, 128, n, 4), np.uint8)
        nib[..., 0::2] = words & 0xF
        nib[..., 1::2] = words >> 4
        vals = E2M1[nib]
    vals = vals * np.repeat(np.exp2(scales.astype(np.float64) - 127.0), 8, axis=1)[..., None]
    return vals.transpose(0, 1, 3, 2).reshape(g * 512, n)


def gelu(v):
    return 0.5 * v * (1.0 + np.tanh(np.sqrt(2.0 / np.pi) * (v + 0.044715 * v**3)))


K, H, T, S, P = 512, 1024, 4096, 1024, 512


def setup_inputs():
    n = np.random.standard_normal
    s = mx_kscale(K)[:, None]
    u = mx_kscale(H)[:, None]
    tab_words, tab_scales = pack_weight(n((K, T)) * s, "e4m3")
    w4_words, w4_scales = pack_weight(0.8 * n((K, H)) / np.sqrt(K) / s, "e2m1")
    return {
        "tab_words": tab_words,
        "tab_scales": tab_scales,
        "offs": striped(np.random.permutation(T)[:S]),
        "w1": (1.5 * n((K, H)) / np.sqrt(K) / s).astype(np.float32),
        "w4_words": w4_words,
        "w4_scales": w4_scales,
        "gain": (np.exp(0.3 * n(H)) * u[:, 0]).astype(np.float32),
        "pos1": striped(np.random.permutation(S)[:P]),
        "w2": (1.7 * n((H, H)) / np.sqrt(H) / u).astype(np.float32),
        "skip": (np.exp(0.3 * n(H)) / u[:, 0]).astype(np.float32),
        "paper": n((H, S)).astype(np.float32),
        "wgo": np.exp(0.3 * n((128, P))).astype(np.float32),
    }


def reference(tab_words, tab_scales, offs, w1, w4_words, w4_scales, gain, pos1, w2, skip, paper, wgo):
    v = unpack_weight(tab_words, tab_scales, "e4m3")[:, unstriped(offs)]
    w4 = unpack_weight(w4_words, w4_scales, "e2m1")
    bent = np.tanh(mxq(f64(w1), 0, "e4m3").T @ v)
    h = f64(gain)[:, None] * (bent + (w4.T @ v))
    x = mxq(h[:, unstriped(pos1)], 0, "e4m3")
    y = mxq(f64(w2), 0, "e4m3").T @ x
    base = f64(skip)[:, None] * h
    y = 1.0 / (1.0 + np.exp(-y)) * base[:, unstriped(pos1)]
    out = np.maximum(base, f64(paper))
    out[:, unstriped(pos1)] = np.tile(f64(wgo), (H // 128, 1)) * y
    return out

@@ -1,0 +1,216 @@
+from contextlib import ExitStack
+
+import concourse.mybir as mybir
+
+K, H, T, S, M = 512, 1024, 4096, 1024, 512
+FLOPS = 2 * (2 * K * H * S + H * H * M)
+
+F32 = mybir.dt.float32
+BF16 = mybir.dt.bfloat16
+I32 = mybir.dt.int32
+U32 = mybir.dt.uint32
+U16 = mybir.dt.uint16
+U8 = mybir.dt.uint8
+FP8X4 = mybir.dt.float8_e4m3fn_x4
+FP4X4 = mybir.dt.float4_e2m1fn_x4
+ACT = mybir.ActivationFunctionType
+ALU = mybir.AluOpType
+
+P = 128
+PACK = 4
+PASS = P * PACK
+BANK = 512
+BLOCKS = H // PASS
+TILES = BLOCKS * PACK
+HALVES = S // BANK
+
+
+def tile_list_giclee_gamut_features_kernel(
+    tc, tab_words, tab_scales, offs, w1, w4_words, w4_scales, gain, pos1, w2, skip, paper, wgo, out
+):
+    nc = tc.nc
+    with ExitStack() as ctx:
+        keep = ctx.enter_context(tc.tile_pool(name="keep", bufs=1))
+        ring = ctx.enter_context(tc.tile_pool(name="ring", bufs=2))
+        psum = ctx.enter_context(tc.psum_pool(name="psum", bufs=4))
+
+        offs_t = keep.tile([P, S // 16], U16, name="offs_t")
+        pos_t = keep.tile([P, M // 16], U16, name="pos_t")
+        tab = keep.tile([P, T], U32, name="tab")
+        tab_s = keep.tile([P, T], U8, name="tab_s")
+        w4_raw = keep.tile([P, 2 * H], U8, name="w4_raw")
+        w4s_raw = keep.tile([P, H], U8, name="w4s_raw")
+        w4_c = keep.tile([P, 2 * H], U8, name="w4_c", align_bytes=64)
+        w4_s = keep.tile([P, H], U8, name="w4_s", align_bytes=64)
+        v_c = [keep.tile([P, BANK], U32, name=f"v_c{h}", align_bytes=64) for h in range(HALVES)]
+        v_s = keep.tile([P, S], U8, name="v_s", align_bytes=64)
+        gain_t = keep.tile([P, BLOCKS, PACK], F32, name="gain_t")
+        skip_t = keep.tile([P, BLOCKS, PACK], F32, name="skip_t")
+        both_t = keep.tile([P, BLOCKS, PACK], F32, name="both_t")
+        wgo_t = keep.tile([P, PACK * M], F32, name="wgo_t")
+        w1_raw = [keep.tile([P, PACK, PASS], F32, name=f"w1_raw{b}") for b in range(BLOCKS)]
+        w2_raw = {(a, b): keep.tile([P, PACK, PASS], F32, name=f"w2_raw{a}{b}") for b in range(BLOCKS) for a in range(BLOCKS)}
+        w1_c = [keep.tile([P, PASS], U32, name=f"w1_c{b}", align_bytes=64) for b in range(BLOCKS)]
+        w1_s = [keep.tile([P, PASS], U8, name=f"w1_s{b}", align_bytes=64) for b in range(BLOCKS)]
+        w2_c = {key: keep.tile([P, PASS], U32, name=f"w2_c{key[0]}{key[1]}", align_bytes=64) for key in w2_raw}
+        w2_s = {key: keep.tile([P, PASS], U8, name=f"w2_s{key[0]}{key[1]}", align_bytes=64) for key in w2_raw}
+        u = [keep.tile([P, S], F32, name=f"u{i}") for i in range(TILES)]
+        page = [keep.tile([P, S], F32, name=f"page{i}") for i in range(TILES)]
+        picked = [keep.tile([P, M], F32, name=f"picked{i}") for i in range(TILES)]
+        x_rows = [keep.tile([P, PACK, M], BF16, name=f"x_rows{b}") for b in range(BLOCKS)]
+        x_c = [keep.tile([P, M], U32, name=f"x_c{b}", align_bytes=64) for b in range(BLOCKS)]
+        x_s = [keep.tile([P, M], U8, name=f"x_s{b}", align_bytes=64) for b in range(BLOCKS)]
+
+        w1_v = w1.rearrange("(p j) c -> p j c", j=PACK)
+        w2_v = w2.rearrange("(a p j) c -> a p j c", a=BLOCKS, j=PACK)
+        paper_v = paper.rearrange("(b p t) j -> b t p j", b=BLOCKS, t=PACK)
+        out_v = out.rearrange("(b p t) j -> b t p j", b=BLOCKS, t=PACK)
+
+        def cols(b):
+            return slice(b * PASS, (b + 1) * PASS)
+
+        nc.vector.memset(tab_s[:].bitcast(I32), 0)
+        nc.vector.memset(w4s_raw[:].bitcast(I32), 0)
+
+        nc.sync.dma_start(out=w1_raw[0][:], in_=w1_v[:, :, cols(0)])
+        for q in range(4):
+            nc.sync.dma_start(out=tab_s[32 * q : 32 * q + 4, :].bitcast(I32), in_=tab_scales[0, 4 * q : 4 * q + 4, :].bitcast(I32))
+        nc.sync.dma_start(offs_t[:], offs)
+        nc.sync.dma_start(out=w4_raw[:].bitcast(I32), in_=w4_words[0].bitcast(I32))
+        nc.sync.dma_start(out=tab[:].bitcast(I32), in_=tab_words[0].rearrange("p t i -> p (t i)").bitcast(I32))
+        for q in range(4):
+            nc.sync.dma_start(out=w4s_raw[32 * q : 32 * q + 4, :].bitcast(I32), in_=w4_scales[0, 4 * q : 4 * q + 4, :].bitcast(I32))
+        nc.sync.dma_start(out=w1_raw[1][:], in_=w1_v[:, :, cols(1)])
+        nc.sync.dma_start(pos_t[:], pos1)
+        nc.sync.dma_start(out=gain_t[:], in_=gain.rearrange("(b p t) -> p b t", b=BLOCKS, t=PACK))
+        nc.sync.dma_start(out=skip_t[:], in_=skip.rearrange("(b p t) -> p b t", b=BLOCKS, t=PACK))
+        for a in range(BLOCKS):
+            nc.sync.dma_start(out=w2_raw[a, 0][:], in_=w2_v[a][:, :, cols(0)])
+        wgo_v = wgo.rearrange("(p t) m -> p (t m)", t=PACK)
+        for q in range(4):
+            nc.sync.dma_start(out=wgo_t[32 * q : 32 * (q + 1), :], in_=wgo_v)
+        for i in range(TILES):
+            nc.sync.dma_start(out=page[i][:], in_=paper_v[i // PACK, i % PACK])
+        for a in range(BLOCKS):
+            nc.sync.dma_start(out=w2_raw[a, 1][:], in_=w2_v[a][:, :, cols(1)])
+
+        def round_weight(copy, raw, parts):
+            grouped = ring.tile([P, PASS * PACK], BF16, name="grouped", align_bytes=64, bufs=4)
+            dst = grouped[:].rearrange("p (t m j) -> p m t j", t=PACK, j=PACK)
+            src = raw[:].rearrange("p j (m t) -> p m t j", t=PACK)
+            step = P // parts
+            for m0 in range(0, P, step):
+                copy(out=dst[:, m0 : m0 + step], in_=src[:, m0 : m0 + step])
+            return grouped
+
+        def quantize(codes, scales, grouped):
+            nc.vector.quantize_mx(out=codes[:].bitcast(FP8X4), scales=scales[:], in_=grouped[:])
+
+        nc.vector.tensor_copy(
+            out=w4_c[:].rearrange("p (b t m e) -> p b m t e", b=BLOCKS, t=PACK, e=2),
+            in_=w4_raw[:].rearrange("p (b m t e) -> p b m t e", b=BLOCKS, t=PACK, e=2),
+        )
+        g0 = round_weight(nc.vector.tensor_copy, w1_raw[0], 1)
+        nc.vector.tensor_copy(out=v_s[:], in_=tab_s[:].indirect(offs_t[:]))
+        quantize(w1_c[0], w1_s[0], g0)
+        nc.vector.tensor_copy(
+            out=w4_s[:].rearrange("p (b t m) -> p b m t", b=BLOCKS, t=PACK),
+            in_=w4s_raw[:].rearrange("p (b m t) -> p b m t", b=BLOCKS, t=PACK),
+        )
+        for h in range(HALVES):
+            nc.vector.tensor_copy(out=v_c[h][:], in_=tab[:].indirect(offs_t[:, h * (BANK // 16) : (h + 1) * (BANK // 16)]))
+
+        def first_stage(i):
+            b, t = divmod(i, PACK)
+            for h in range(HALVES):
+                js = slice(h * BANK, (h + 1) * BANK)
+                bent = psum.tile([P, BANK], F32, name="bent")
+                nc.tensor.matmul_mx(
+                    out=bent[:],
+                    lhsT=w1_c[b][:, t * P : (t + 1) * P].bitcast(FP8X4),
+                    lhsT_scale=w1_s[b][:, t * P : (t + 1) * P],
+                    rhs=v_c[h][:].bitcast(FP8X4),
+                    rhs_scale=v_s[:, js],
+                    start=True,
+                    stop=True,
+                )
+                flat = psum.tile([P, BANK], F32, name="flat")
+                nc.tensor.matmul_mx(
+                    out=flat[:],
+                    lhsT=w4_c[:, 2 * P * i : 2 * P * (i + 1)].bitcast(FP4X4),
+                    lhsT_scale=w4_s[:, P * i : P * (i + 1)],
+                    rhs=v_c[h][:].bitcast(FP8X4),
+                    rhs_scale=v_s[:, js],
+                    start=True,
+                    stop=True,
+                )
+                nc.scalar.activation(out=u[i][:, js], in_=bent[:], func=ACT.Tanh)
+                nc.vector.tensor_tensor(out=u[i][:, js], in0=flat[:], in1=u[i][:, js], op=ALU.add)
+
+        def pick(i):
+            nc.vector.tensor_copy(out=picked[i][:], in_=u[i][:].indirect(pos_t[:]))
+
+        def round_picked(i):
+            b, t = divmod(i, PACK)
+            nc.scalar.activation(out=x_rows[b][:, t, :], in_=picked[i][:], func=ACT.Copy, scale=gain_t[:, b, t : t + 1])
+
+        def weave_picked(b):
+            grouped = ring.tile([P, PASS * PACK], BF16, name="grouped", align_bytes=64, bufs=4)
+            nc.scalar.copy(
+                out=grouped[:].rearrange("p (c i t) -> p c t i", i=4, t=PACK),
+                in_=x_rows[b][:].rearrange("p t (c i) -> p c t i", i=4),
+            )
+            quantize(x_c[b], x_s[b], grouped)
+
+        first_stage(0)
+        g1 = round_weight(nc.scalar.copy, w1_raw[1], 2)
+        quantize(w1_c[1], w1_s[1], g1)
+        for i in range(1, TILES):
+            first_stage(i)
+            pick(i - 1)
+        pick(TILES - 1)
+        for b in range(BLOCKS):
+            for t in range(PACK):
+                round_picked(b * PACK + t)
+            weave_picked(b)
+            quantize(w2_c[b, 0], w2_s[b, 0], round_weight(nc.scalar.copy, w2_raw[b, 0], 2))
+
+        nc.vector.tensor_tensor(out=both_t[:], in0=gain_t[:], in1=skip_t[:], op=ALU.mult)
+
+        def floor_page(i):
+            b, t = divmod(i, PACK)
+            nc.vector.scalar_tensor_tensor(
+                out=page[i][:], in0=u[i][:], scalar=both_t[:, b, t : t + 1], in1=page[i][:], op0=ALU.mult, op1=ALU.max
+            )
+
+        def weigh_picked(i):
+            b, t = divmod(i, PACK)
+            nc.vector.scalar_tensor_tensor(
+                out=picked[i][:], in0=picked[i][:], scalar=both_t[:, b, t : t + 1], in1=wgo_t[:, t * M : (t + 1) * M], op0=ALU.mult, op1=ALU.mult
+            )
+
+        def second_stage(i):
+            b, t = divmod(i, PACK)
+            y = psum.tile([P, BANK], F32, name="bent")
+            for a in range(BLOCKS):
+                nc.tensor.matmul_mx(
+                    out=y[:],
+                    lhsT=w2_c[a, b][:, t * P : (t + 1) * P].bitcast(FP8X4),
+                    lhsT_scale=w2_s[a, b][:, t * P : (t + 1) * P],
+                    rhs=x_c[a][:].bitcast(FP8X4),
+                    rhs_scale=x_s[a][:],
+                    start=(a == 0),
+                    stop=(a == BLOCKS - 1),
+                )
+            gate = ring.tile([P, M], F32, name="gate", bufs=4)
+            nc.scalar.activation(out=gate[:], in_=y[:], func=ACT.Sigmoid)
+            weigh_picked(i)
+            floor_page(i)
+            nc.vector.tensor_tensor(out=page[i][:].indirect(pos_t[:]), in0=gate[:], in1=picked[i][:], op=ALU.mult)
+            nc.sync.dma_start(out=out_v[b, t], in_=page[i][:])
+
+        for i in range(TILES):
+            if i == PACK:
+                for a in range(BLOCKS):
+                    quantize(w2_c[a, 1], w2_s[a, 1], round_weight(nc.scalar.copy, w2_raw[a, 1], 2))
+            second_stage(i)

@@ -46,19 +46,19 @@ def tile_list_giclee_gamut_features_kernel(
         v_s = keep.tile([P, S], U8, name="v_s", align_bytes=64)
         gain_t = keep.tile([P, BLOCKS, PACK], F32, name="gain_t")
         skip_t = keep.tile([P, BLOCKS, PACK], F32, name="skip_t")
-        both_t = keep.tile([P, BLOCKS, PACK], F32, name="both_t")
+        half_t = keep.tile([P, BLOCKS, PACK], F32, name="half_t")
         wgo_t = keep.tile([P, PACK * M], F32, name="wgo_t")
-        w1_raw = [keep.tile([P, PACK, PASS], F32, name=f"w1_raw{b}") for b in range(BLOCKS)]
-        w2_raw = {(a, b): keep.tile([P, PACK, PASS], F32, name=f"w2_raw{a}{b}") for b in range(BLOCKS) for a in range(BLOCKS)}
+        w1_raw = [keep.tile([P, PACK, PASS], F32, name=f"w1_raw{b}", tag=f"w1_raw{b}", align_bytes=64) for b in range(BLOCKS)]
+        w2_raw = {(a, b): keep.tile([P, PACK, PASS], F32, name=f"w2_raw{a}{b}", tag=f"w2_raw{a}{b}", align_bytes=64) for b in range(BLOCKS) for a in range(BLOCKS)}
         w1_c = [keep.tile([P, PASS], U32, name=f"w1_c{b}", align_bytes=64) for b in range(BLOCKS)]
         w1_s = [keep.tile([P, PASS], U8, name=f"w1_s{b}", align_bytes=64) for b in range(BLOCKS)]
-        w2_c = {key: keep.tile([P, PASS], U32, name=f"w2_c{key[0]}{key[1]}", align_bytes=64) for key in w2_raw}
+        w2_c = {key: keep.tile([P, PASS], U32, name=f"w2_c{key[0]}{key[1]}", align_bytes=64) for key in w2_raw if key[1] == 0}
         w2_s = {key: keep.tile([P, PASS], U8, name=f"w2_s{key[0]}{key[1]}", align_bytes=64) for key in w2_raw}
-        u = [keep.tile([P, S], F32, name=f"u{i}") for i in range(TILES)]
+        u = [keep.tile([P, S], F32, name=f"u{i}", tag=f"u{i}", align_bytes=64) for i in range(TILES)]
         page = [keep.tile([P, S], F32, name=f"page{i}") for i in range(TILES)]
-        picked = [keep.tile([P, M], F32, name=f"picked{i}") for i in range(TILES)]
-        x_rows = [keep.tile([P, PACK, M], BF16, name=f"x_rows{b}") for b in range(BLOCKS)]
-        x_c = [keep.tile([P, M], U32, name=f"x_c{b}", align_bytes=64) for b in range(BLOCKS)]
+        picked = {}
+        x_rows = {}
+        x_c = [keep.tile([P, M], U32, name="x_c0", align_bytes=64)]
         x_s = [keep.tile([P, M], U8, name=f"x_s{b}", align_bytes=64) for b in range(BLOCKS)]
 
         w1_v = w1.rearrange("(p j) c -> p j c", j=PACK)
@@ -82,26 +82,39 @@ def tile_list_giclee_gamut_features_kernel(
             nc.sync.dma_start(out=w4s_raw[32 * q : 32 * q + 4, :].bitcast(I32), in_=w4_scales[0, 4 * q : 4 * q + 4, :].bitcast(I32))
         nc.sync.dma_start(out=w1_raw[1][:], in_=w1_v[:, :, cols(1)])
         nc.sync.dma_start(pos_t[:], pos1)
+        nc.sync.dma_start(out=w2_raw[0, 0][:], in_=w2_v[0][:, :, cols(0)])
         nc.sync.dma_start(out=gain_t[:], in_=gain.rearrange("(b p t) -> p b t", b=BLOCKS, t=PACK))
         nc.sync.dma_start(out=skip_t[:], in_=skip.rearrange("(b p t) -> p b t", b=BLOCKS, t=PACK))
-        for a in range(BLOCKS):
-            nc.sync.dma_start(out=w2_raw[a, 0][:], in_=w2_v[a][:, :, cols(0)])
+        nc.sync.dma_start(out=w2_raw[1, 0][:], in_=w2_v[1][:, :, cols(0)])
         wgo_v = wgo.rearrange("(p t) m -> p (t m)", t=PACK)
         for q in range(4):
             nc.sync.dma_start(out=wgo_t[32 * q : 32 * (q + 1), :], in_=wgo_v)
-        for i in range(TILES):
-            nc.sync.dma_start(out=page[i][:], in_=paper_v[i // PACK, i % PACK])
-        for a in range(BLOCKS):
-            nc.sync.dma_start(out=w2_raw[a, 1][:], in_=w2_v[a][:, :, cols(1)])
+        for b in range(BLOCKS):
+            for t in range(PACK):
+                nc.sync.dma_start(out=page[b * PACK + t][:], in_=paper_v[b, t])
+            nc.sync.dma_start(out=w2_raw[b, 1][:], in_=w2_v[b][:, :, cols(1)])
 
-        def round_weight(copy, raw, parts):
-            grouped = ring.tile([P, PASS * PACK], BF16, name="grouped", align_bytes=64, bufs=4)
+        def new_grouped(tag=None):
+            if tag is None:
+                return ring.tile([P, PASS * PACK], BF16, name="grouped", align_bytes=64, bufs=3)
+            return keep.tile([P, PASS * PACK], BF16, name="grouped", align_bytes=64, tag=tag)
+
+        def round_weight(copy, grouped, raw, m0, m1):
             dst = grouped[:].rearrange("p (t m j) -> p m t j", t=PACK, j=PACK)
             src = raw[:].rearrange("p j (m t) -> p m t j", t=PACK)
-            step = P // parts
-            for m0 in range(0, P, step):
-                copy(out=dst[:, m0 : m0 + step], in_=src[:, m0 : m0 + step])
-            return grouped
+            copy(out=dst[:, m0:m1], in_=src[:, m0:m1])
+
+        def weight_steps(codes, scales, raw, tag=None):
+            grouped = new_grouped(tag)
+
+            def first():
+                round_weight(nc.scalar.copy, grouped, raw, 0, P // 2)
+
+            def second():
+                round_weight(nc.scalar.copy, grouped, raw, P // 2, P)
+                quantize(codes, scales, grouped)
+
+            return [first, second]
 
         def quantize(codes, scales, grouped):
             nc.vector.quantize_mx(out=codes[:].bitcast(FP8X4), scales=scales[:], in_=grouped[:])
@@ -110,7 +123,8 @@ def tile_list_giclee_gamut_features_kernel(
             out=w4_c[:].rearrange("p (b t m e) -> p b m t e", b=BLOCKS, t=PACK, e=2),
             in_=w4_raw[:].rearrange("p (b m t e) -> p b m t e", b=BLOCKS, t=PACK, e=2),
         )
-        g0 = round_weight(nc.vector.tensor_copy, w1_raw[0], 1)
+        g0 = new_grouped()
+        round_weight(nc.vector.tensor_copy, g0, w1_raw[0], 0, P)
         nc.vector.tensor_copy(out=v_s[:], in_=tab_s[:].indirect(offs_t[:]))
         quantize(w1_c[0], w1_s[0], g0)
         nc.vector.tensor_copy(
@@ -120,7 +134,7 @@ def tile_list_giclee_gamut_features_kernel(
         for h in range(HALVES):
             nc.vector.tensor_copy(out=v_c[h][:], in_=tab[:].indirect(offs_t[:, h * (BANK // 16) : (h + 1) * (BANK // 16)]))
 
-        def first_stage(i):
+        def first_stage(i, tag):
             b, t = divmod(i, PACK)
             for h in range(HALVES):
                 js = slice(h * BANK, (h + 1) * BANK)
@@ -144,50 +158,85 @@ def tile_list_giclee_gamut_features_kernel(
                     start=True,
                     stop=True,
                 )
-                nc.scalar.activation(out=u[i][:, js], in_=bent[:], func=ACT.Tanh)
-                nc.vector.tensor_tensor(out=u[i][:, js], in0=flat[:], in1=u[i][:, js], op=ALU.add)
+                bent_sb = keep.tile([P, BANK], F32, name="bent_sb", tag=(f"lead{i}", tag)[h], align_bytes=64)
+                nc.scalar.activation(out=bent_sb[:], in_=bent[:], func=ACT.Tanh)
+                nc.vector.tensor_tensor(out=u[i][:, js], in0=flat[:], in1=bent_sb[:], op=ALU.add)
 
         def pick(i):
+            b, t = divmod(i, PACK)
+            picked[i] = keep.tile([P, M], F32, name="picked", tag=f"lead{(i + 1) % TILES}", align_bytes=64)
             nc.vector.tensor_copy(out=picked[i][:], in_=u[i][:].indirect(pos_t[:]))
+            engine = nc.vector if i == TILES - 1 else nc.gpsimd
+            engine.tensor_tensor(out=weighed[b][:, t, :], in0=picked[i][:], in1=wgo_t[:, t * M : (t + 1) * M], op=ALU.mult)
 
         def round_picked(i):
             b, t = divmod(i, PACK)
             nc.scalar.activation(out=x_rows[b][:, t, :], in_=picked[i][:], func=ACT.Copy, scale=gain_t[:, b, t : t + 1])
 
-        def weave_picked(b):
-            grouped = ring.tile([P, PASS * PACK], BF16, name="grouped", align_bytes=64, bufs=4)
+        def weave_picked(b, tag=None):
+            grouped = new_grouped(tag)
             nc.scalar.copy(
                 out=grouped[:].rearrange("p (c i t) -> p c t i", i=4, t=PACK),
                 in_=x_rows[b][:].rearrange("p t (c i) -> p c t i", i=4),
             )
-            quantize(x_c[b], x_s[b], grouped)
+            return grouped
 
-        first_stage(0)
-        g1 = round_weight(nc.scalar.copy, w1_raw[1], 2)
-        quantize(w1_c[1], w1_s[1], g1)
-        for i in range(1, TILES):
-            first_stage(i)
-            pick(i - 1)
-        pick(TILES - 1)
-        for b in range(BLOCKS):
+        def row_factors(b, tag):
+            factors = keep.tile([P, PACK], F32, name=f"both{b}", tag=tag, align_bytes=64)
+            nc.vector.tensor_tensor(out=factors[:], in0=gain_t[:, b, :], in1=skip_t[:, b, :], op=ALU.mult)
+            return factors
+
+        def floor_pages(b):
             for t in range(PACK):
-                round_picked(b * PACK + t)
-            weave_picked(b)
-            quantize(w2_c[b, 0], w2_s[b, 0], round_weight(nc.scalar.copy, w2_raw[b, 0], 2))
+                i = b * PACK + t
+                nc.vector.scalar_tensor_tensor(
+                    out=page[i][:], in0=u[i][:], scalar=both[b][:, t : t + 1], in1=page[i][:], op0=ALU.mult, op1=ALU.max
+                )
 
-        nc.vector.tensor_tensor(out=both_t[:], in0=gain_t[:], in1=skip_t[:], op=ALU.mult)
+        weighed = [None, None]
+        weighed[0] = keep.tile([P, PACK, M], F32, name="weighed0", tag="w1_raw0", align_bytes=64)
 
-        def floor_page(i):
-            b, t = divmod(i, PACK)
-            nc.vector.scalar_tensor_tensor(
-                out=page[i][:], in0=u[i][:], scalar=both_t[:, b, t : t + 1], in1=page[i][:], op0=ALU.mult, op1=ALU.max
-            )
-
-        def weigh_picked(i):
-            b, t = divmod(i, PACK)
-            nc.vector.scalar_tensor_tensor(
-                out=picked[i][:], in0=picked[i][:], scalar=both_t[:, b, t : t + 1], in1=wgo_t[:, t * M : (t + 1) * M], op0=ALU.mult, op1=ALU.mult
-            )
+        first_stage(0, "trail_a")
+        first_stage(1, "trail_b")
+        pick(0)
+        for step in weight_steps(w1_c[1], w1_s[1], w1_raw[1]):
+            step()
+        first_stage(2, "w1_raw1")
+        weighed[1] = keep.tile([P, PACK, M], F32, name="weighed1", tag="w1_raw1", align_bytes=64)
+        pick(1)
+        first_stage(3, "trail_a")
+        pick(2)
+        for step in weight_steps(w2_c[0, 0], w2_s[0, 0], w2_raw[0, 0]):
+            step()
+        first_stage(4, "w2_raw00")
+        pick(3)
+        first_stage(5, "trail_b")
+        pick(4)
+        for step in weight_steps(w2_c[1, 0], w2_s[1, 0], w2_raw[1, 0], "x_rows1"):
+            step()
+        first_stage(6, "w2_raw10")
+        pick(5)
+        first_stage(7, "trail_a")
+        pick(6)
+        both = [row_factors(0, "trail_a")]
+        pick(7)
+        x_rows[0] = keep.tile([P, PACK, M], BF16, name="x_rows0", tag="w2_raw10", align_bytes=64)
+        x_rows[1] = keep.tile([P, PACK, M], BF16, name="x_rows1", tag="x_rows1", align_bytes=64)
+        for i in range(PACK):
+            round_picked(i)
+        quantize(x_c[0], x_s[0], weave_picked(0))
+        for i in range(PACK, TILES):
+            round_picked(i)
+        grouped1 = weave_picked(1, "woven1")
+        floor_pages(0)
+        x_c.append(keep.tile([P, M], U32, name="x_c1", tag="u2", align_bytes=64))
+        quantize(x_c[1], x_s[1], grouped1)
+        both.append(row_factors(1, "woven1"))
+        nc.vector.scalar_tensor_tensor(out=half_t[:], in0=gain_t[:], scalar=0.5, in1=skip_t[:], op0=ALU.mult, op1=ALU.mult)
+        floor_pages(1)
+        w2_c[0, 1] = keep.tile([P, PASS], U32, name="w2_c01", tag="u4", align_bytes=64)
+        for step in weight_steps(w2_c[0, 1], w2_s[0, 1], w2_raw[0, 1], "x_rows1"):
+            step()
 
         def second_stage(i):
             b, t = divmod(i, PACK)
@@ -202,15 +251,21 @@ def tile_list_giclee_gamut_features_kernel(
                     start=(a == 0),
                     stop=(a == BLOCKS - 1),
                 )
-            gate = ring.tile([P, M], F32, name="gate", bufs=4)
-            nc.scalar.activation(out=gate[:], in_=y[:], func=ACT.Sigmoid)
-            weigh_picked(i)
-            floor_page(i)
-            nc.vector.tensor_tensor(out=page[i][:].indirect(pos_t[:]), in0=gate[:], in1=picked[i][:], op=ALU.mult)
+            gate = ring.tile([P, M], F32, name="gate", bufs=2)
+            nc.scalar.activation(out=gate[:], in_=y[:], func=ACT.Tanh, scale=0.5)
+            if i == 0:
+                scaled = keep.tile([P, M], F32, name="scaled0", tag="u5", align_bytes=64)
+            elif i == 2:
+                scaled = keep.tile([P, M], F32, name="scaled2", tag="x_rows1", align_bytes=64)
+            else:
+                scaled = ring.tile([P, M], F32, name="scaled", bufs=3)
+            nc.scalar.activation(out=scaled[:], in_=gate[:], func=ACT.Identity, scale=half_t[:, b, t : t + 1], bias=half_t[:, b, t : t + 1])
+            nc.vector.tensor_tensor(out=page[i][:].indirect(pos_t[:]), in0=scaled[:], in1=weighed[b][:, t, :], op=ALU.mult)
             nc.sync.dma_start(out=out_v[b, t], in_=page[i][:])
 
         for i in range(TILES):
-            if i == PACK:
-                for a in range(BLOCKS):
-                    quantize(w2_c[a, 1], w2_s[a, 1], round_weight(nc.scalar.copy, w2_raw[a, 1], 2))
             second_stage(i)
+            if i == 0:
+                w2_c[1, 1] = keep.tile([P, PASS], U32, name="w2_c11", tag="u5", align_bytes=64)
+                for step in weight_steps(w2_c[1, 1], w2_s[1, 1], w2_raw[1, 1], "x_rows1"):
+                    step()

@@ -23,6 +23,7 @@ BANK = 512
 BLOCKS = H // PASS
 TILES = BLOCKS * PACK
 HALVES = S // BANK
+EARLY = 5
 
 
 def tile_list_giclee_gamut_features_kernel(
@@ -44,9 +45,9 @@ def tile_list_giclee_gamut_features_kernel(
         w4_s = keep.tile([P, H], U8, name="w4_s", align_bytes=64)
         v_c = [keep.tile([P, BANK], U32, name=f"v_c{h}", align_bytes=64) for h in range(HALVES)]
         v_s = keep.tile([P, S], U8, name="v_s", align_bytes=64)
-        gain_t = keep.tile([P, BLOCKS, PACK], F32, name="gain_t")
-        skip_t = keep.tile([P, BLOCKS, PACK], F32, name="skip_t")
-        half_t = keep.tile([P, BLOCKS, PACK], F32, name="half_t")
+        gain_t = keep.tile([P, TILES], F32, name="gain_t")
+        skip_t = keep.tile([P, TILES], F32, name="skip_t")
+        half_t = keep.tile([P, TILES], F32, name="half_t")
         wgo_t = keep.tile([P, PACK * M], F32, name="wgo_t")
         w1_raw = [keep.tile([P, PACK, PASS], F32, name=f"w1_raw{b}", tag=f"w1_raw{b}", align_bytes=64) for b in range(BLOCKS)]
         w2_raw = {(a, b): keep.tile([P, PACK, PASS], F32, name=f"w2_raw{a}{b}", tag=f"w2_raw{a}{b}", align_bytes=64) for b in range(BLOCKS) for a in range(BLOCKS)}
@@ -70,7 +71,7 @@ def tile_list_giclee_gamut_features_kernel(
             return slice(b * PASS, (b + 1) * PASS)
 
         nc.vector.memset(tab_s[:].bitcast(I32), 0)
-        nc.vector.memset(w4s_raw[:].bitcast(I32), 0)
+        nc.gpsimd.memset(w4s_raw[:].bitcast(I32), 0)
 
         nc.sync.dma_start(out=w1_raw[0][:], in_=w1_v[:, :, cols(0)])
         for q in range(4):
@@ -79,12 +80,12 @@ def tile_list_giclee_gamut_features_kernel(
         nc.sync.dma_start(out=w4_raw[:].bitcast(I32), in_=w4_words[0].bitcast(I32))
         nc.sync.dma_start(out=tab[:].bitcast(I32), in_=tab_words[0].rearrange("p t i -> p (t i)").bitcast(I32))
         for q in range(4):
-            nc.sync.dma_start(out=w4s_raw[32 * q : 32 * q + 4, :].bitcast(I32), in_=w4_scales[0, 4 * q : 4 * q + 4, :].bitcast(I32))
+            nc.gpsimd.dma_start(out=w4s_raw[32 * q : 32 * q + 4, :].bitcast(I32), in_=w4_scales[0, 4 * q : 4 * q + 4, :].bitcast(I32))
         nc.sync.dma_start(out=w1_raw[1][:], in_=w1_v[:, :, cols(1)])
         nc.sync.dma_start(pos_t[:], pos1)
         nc.sync.dma_start(out=w2_raw[0, 0][:], in_=w2_v[0][:, :, cols(0)])
-        nc.sync.dma_start(out=gain_t[:], in_=gain.rearrange("(b p t) -> p b t", b=BLOCKS, t=PACK))
-        nc.sync.dma_start(out=skip_t[:], in_=skip.rearrange("(b p t) -> p b t", b=BLOCKS, t=PACK))
+        nc.sync.dma_start(out=gain_t[:].rearrange("p (b t) -> p b t", t=PACK), in_=gain.rearrange("(b p t) -> p b t", b=BLOCKS, t=PACK))
+        nc.sync.dma_start(out=skip_t[:].rearrange("p (b t) -> p b t", t=PACK), in_=skip.rearrange("(b p t) -> p b t", b=BLOCKS, t=PACK))
         nc.sync.dma_start(out=w2_raw[1, 0][:], in_=w2_v[1][:, :, cols(0)])
         wgo_v = wgo.rearrange("(p t) m -> p (t m)", t=PACK)
         for q in range(4):
@@ -138,7 +139,7 @@ def tile_list_giclee_gamut_features_kernel(
             b, t = divmod(i, PACK)
             for h in range(HALVES):
                 js = slice(h * BANK, (h + 1) * BANK)
-                bent = psum.tile([P, BANK], F32, name="bent")
+                bent = psum.tile([P, BANK], F32, name="bent", bufs=2)
                 nc.tensor.matmul_mx(
                     out=bent[:],
                     lhsT=w1_c[b][:, t * P : (t + 1) * P].bitcast(FP8X4),
@@ -148,7 +149,7 @@ def tile_list_giclee_gamut_features_kernel(
                     start=True,
                     stop=True,
                 )
-                flat = psum.tile([P, BANK], F32, name="flat")
+                flat = psum.tile([P, BANK], F32, name="flat", bufs=6)
                 nc.tensor.matmul_mx(
                     out=flat[:],
                     lhsT=w4_c[:, 2 * P * i : 2 * P * (i + 1)].bitcast(FP4X4),
@@ -171,7 +172,7 @@ def tile_list_giclee_gamut_features_kernel(
 
         def round_picked(i):
             b, t = divmod(i, PACK)
-            nc.scalar.activation(out=x_rows[b][:, t, :], in_=picked[i][:], func=ACT.Copy, scale=gain_t[:, b, t : t + 1])
+            nc.scalar.activation(out=x_rows[b][:, t, :], in_=picked[i][:], func=ACT.Copy, scale=gain_t[:, i : i + 1])
 
         def weave_picked(b, tag=None):
             grouped = new_grouped(tag)
@@ -181,16 +182,15 @@ def tile_list_giclee_gamut_features_kernel(
             )
             return grouped
 
-        def row_factors(b, tag):
-            factors = keep.tile([P, PACK], F32, name=f"both{b}", tag=tag, align_bytes=64)
-            nc.vector.tensor_tensor(out=factors[:], in0=gain_t[:, b, :], in1=skip_t[:, b, :], op=ALU.mult)
+        def row_factors(i0, i1, tag):
+            factors = keep.tile([P, i1 - i0], F32, name="factors", tag=tag, align_bytes=64)
+            nc.vector.tensor_tensor(out=factors[:], in0=gain_t[:, i0:i1], in1=skip_t[:, i0:i1], op=ALU.mult)
             return factors
 
-        def floor_pages(b):
-            for t in range(PACK):
-                i = b * PACK + t
+        def floor_pages(i0, i1, factors):
+            for i in range(i0, i1):
                 nc.vector.scalar_tensor_tensor(
-                    out=page[i][:], in0=u[i][:], scalar=both[b][:, t : t + 1], in1=page[i][:], op0=ALU.mult, op1=ALU.max
+                    out=page[i][:], in0=u[i][:], scalar=factors[:, i - i0 : i - i0 + 1], in1=page[i][:], op0=ALU.mult, op1=ALU.max
                 )
 
         weighed = [None, None]
@@ -199,28 +199,28 @@ def tile_list_giclee_gamut_features_kernel(
         first_stage(0, "trail_a")
         first_stage(1, "trail_b")
         pick(0)
+        first_stage(2, "trail_c")
+        pick(1)
         for step in weight_steps(w1_c[1], w1_s[1], w1_raw[1]):
             step()
-        first_stage(2, "w1_raw1")
+        first_stage(3, "w1_raw1")
         weighed[1] = keep.tile([P, PACK, M], F32, name="weighed1", tag="w1_raw1", align_bytes=64)
-        pick(1)
-        first_stage(3, "trail_a")
         pick(2)
+        first_stage(4, "trail_a")
+        pick(3)
         for step in weight_steps(w2_c[0, 0], w2_s[0, 0], w2_raw[0, 0]):
             step()
-        first_stage(4, "w2_raw00")
-        pick(3)
-        first_stage(5, "trail_b")
+        first_stage(5, "w2_raw00")
         pick(4)
+        first_stage(6, "trail_b")
+        pick(5)
         for step in weight_steps(w2_c[1, 0], w2_s[1, 0], w2_raw[1, 0], "x_rows1"):
             step()
-        first_stage(6, "w2_raw10")
-        pick(5)
-        first_stage(7, "trail_a")
+        first_stage(7, "w2_raw10")
         pick(6)
-        both = [row_factors(0, "trail_a")]
+        early = row_factors(0, EARLY, "w2_raw10")
         pick(7)
-        x_rows[0] = keep.tile([P, PACK, M], BF16, name="x_rows0", tag="w2_raw10", align_bytes=64)
+        x_rows[0] = keep.tile([P, PACK, M], BF16, name="x_rows0", tag="trail_b", align_bytes=64)
         x_rows[1] = keep.tile([P, PACK, M], BF16, name="x_rows1", tag="x_rows1", align_bytes=64)
         for i in range(PACK):
             round_picked(i)
@@ -228,19 +228,16 @@ def tile_list_giclee_gamut_features_kernel(
         for i in range(PACK, TILES):
             round_picked(i)
         grouped1 = weave_picked(1, "woven1")
-        floor_pages(0)
-        x_c.append(keep.tile([P, M], U32, name="x_c1", tag="u2", align_bytes=64))
+        floor_pages(0, EARLY, early)
+        x_c.append(keep.tile([P, M], U32, name="x_c1", tag="u3", align_bytes=64))
         quantize(x_c[1], x_s[1], grouped1)
-        both.append(row_factors(1, "woven1"))
+        late = row_factors(EARLY, TILES, "woven1")
         nc.vector.scalar_tensor_tensor(out=half_t[:], in0=gain_t[:], scalar=0.5, in1=skip_t[:], op0=ALU.mult, op1=ALU.mult)
-        floor_pages(1)
-        w2_c[0, 1] = keep.tile([P, PASS], U32, name="w2_c01", tag="u4", align_bytes=64)
-        for step in weight_steps(w2_c[0, 1], w2_s[0, 1], w2_raw[0, 1], "x_rows1"):
-            step()
+        floor_pages(EARLY, TILES, late)
 
         def second_stage(i):
             b, t = divmod(i, PACK)
-            y = psum.tile([P, BANK], F32, name="bent")
+            y = psum.tile([P, BANK], F32, name="flat", bufs=6)
             for a in range(BLOCKS):
                 nc.tensor.matmul_mx(
                     out=y[:],
@@ -253,19 +250,19 @@ def tile_list_giclee_gamut_features_kernel(
                 )
             gate = ring.tile([P, M], F32, name="gate", bufs=2)
             nc.scalar.activation(out=gate[:], in_=y[:], func=ACT.Tanh, scale=0.5)
-            if i == 0:
-                scaled = keep.tile([P, M], F32, name="scaled0", tag="u5", align_bytes=64)
-            elif i == 2:
-                scaled = keep.tile([P, M], F32, name="scaled2", tag="x_rows1", align_bytes=64)
+            if i < BLOCKS:
+                scaled = keep.tile([P, M], F32, name="scaled", tag=f"u{6 + i}", align_bytes=64)
+            elif i == 3:
+                scaled = keep.tile([P, M], F32, name="scaled", tag="x_rows1", align_bytes=64)
             else:
                 scaled = ring.tile([P, M], F32, name="scaled", bufs=3)
-            nc.scalar.activation(out=scaled[:], in_=gate[:], func=ACT.Identity, scale=half_t[:, b, t : t + 1], bias=half_t[:, b, t : t + 1])
+            nc.scalar.activation(out=scaled[:], in_=gate[:], func=ACT.Identity, scale=half_t[:, i : i + 1], bias=half_t[:, i : i + 1])
             nc.vector.tensor_tensor(out=page[i][:].indirect(pos_t[:]), in0=scaled[:], in1=weighed[b][:, t, :], op=ALU.mult)
             nc.sync.dma_start(out=out_v[b, t], in_=page[i][:])
 
         for i in range(TILES):
             second_stage(i)
-            if i == 0:
-                w2_c[1, 1] = keep.tile([P, PASS], U32, name="w2_c11", tag="u5", align_bytes=64)
-                for step in weight_steps(w2_c[1, 1], w2_s[1, 1], w2_raw[1, 1], "x_rows1"):
+            if i < BLOCKS:
+                w2_c[i, 1] = keep.tile([P, PASS], U32, name="w2_c", tag=f"u{6 + i}", align_bytes=64)
+                for step in weight_steps(w2_c[i, 1], w2_s[i, 1], w2_raw[i, 1], "x_rows1"):
                     step()

@@ -42,7 +42,7 @@ def tile_list_giclee_gamut_features_kernel(
         w4_raw = keep.tile([P, 2 * H], U8, name="w4_raw")
         w4s_raw = keep.tile([P, H], U8, name="w4s_raw")
         w4_c = keep.tile([P, 2 * H], U8, name="w4_c", align_bytes=64)
-        w4_s = keep.tile([P, H], U8, name="w4_s", align_bytes=64)
+        w4_s = [keep.tile([P, P], U8, name=f"w4_s{i}", align_bytes=64) for i in range(TILES)]
         v_c = [keep.tile([P, BANK], U32, name=f"v_c{h}", align_bytes=64) for h in range(HALVES)]
         v_s = keep.tile([P, S], U8, name="v_s", align_bytes=64)
         gain_t = keep.tile([P, TILES], F32, name="gain_t")
@@ -80,7 +80,7 @@ def tile_list_giclee_gamut_features_kernel(
         nc.sync.dma_start(out=w4_raw[:].bitcast(I32), in_=w4_words[0].bitcast(I32))
         nc.sync.dma_start(out=tab[:].bitcast(I32), in_=tab_words[0].rearrange("p t i -> p (t i)").bitcast(I32))
         for q in range(4):
-            nc.gpsimd.dma_start(out=w4s_raw[32 * q : 32 * q + 4, :].bitcast(I32), in_=w4_scales[0, 4 * q : 4 * q + 4, :].bitcast(I32))
+            nc.sync.dma_start(out=w4s_raw[32 * q : 32 * q + 4, :].bitcast(I32), in_=w4_scales[0, 4 * q : 4 * q + 4, :].bitcast(I32))
         nc.sync.dma_start(out=w1_raw[1][:], in_=w1_v[:, :, cols(1)])
         nc.sync.dma_start(pos_t[:], pos1)
         nc.sync.dma_start(out=w2_raw[0, 0][:], in_=w2_v[0][:, :, cols(0)])
@@ -121,17 +121,16 @@ def tile_list_giclee_gamut_features_kernel(
             nc.vector.quantize_mx(out=codes[:].bitcast(FP8X4), scales=scales[:], in_=grouped[:])
 
         nc.vector.tensor_copy(
-            out=w4_c[:].rearrange("p (b t m e) -> p b m t e", b=BLOCKS, t=PACK, e=2),
-            in_=w4_raw[:].rearrange("p (b m t e) -> p b m t e", b=BLOCKS, t=PACK, e=2),
+            out=w4_c[:].bitcast(U16).rearrange("p (b t m) -> p b m t", b=BLOCKS, t=PACK),
+            in_=w4_raw[:].bitcast(U16).rearrange("p (b m t) -> p b m t", b=BLOCKS, t=PACK),
         )
         g0 = new_grouped()
         round_weight(nc.vector.tensor_copy, g0, w1_raw[0], 0, P)
         nc.vector.tensor_copy(out=v_s[:], in_=tab_s[:].indirect(offs_t[:]))
         quantize(w1_c[0], w1_s[0], g0)
-        nc.vector.tensor_copy(
-            out=w4_s[:].rearrange("p (b t m) -> p b m t", b=BLOCKS, t=PACK),
-            in_=w4s_raw[:].rearrange("p (b m t) -> p b m t", b=BLOCKS, t=PACK),
-        )
+        w4s_dealt = w4s_raw[:].rearrange("p (b m t) -> p b t m", b=BLOCKS, t=PACK)
+        for i in range(TILES):
+            nc.gpsimd.tensor_copy(out=w4_s[i][:], in_=w4s_dealt[:, i // PACK, i % PACK, :])
         for h in range(HALVES):
             nc.vector.tensor_copy(out=v_c[h][:], in_=tab[:].indirect(offs_t[:, h * (BANK // 16) : (h + 1) * (BANK // 16)]))
 
@@ -153,7 +152,7 @@ def tile_list_giclee_gamut_features_kernel(
                 nc.tensor.matmul_mx(
                     out=flat[:],
                     lhsT=w4_c[:, 2 * P * i : 2 * P * (i + 1)].bitcast(FP4X4),
-                    lhsT_scale=w4_s[:, P * i : P * (i + 1)],
+                    lhsT_scale=w4_s[i][:],
                     rhs=v_c[h][:].bitcast(FP8X4),
                     rhs_scale=v_s[:, js],
                     start=True,

@@ -58,7 +58,7 @@ def tile_list_giclee_gamut_features_kernel(
         u = [keep.tile([P, S], F32, name=f"u{i}", tag=f"u{i}", align_bytes=64) for i in range(TILES)]
         page = [keep.tile([P, S], F32, name=f"page{i}") for i in range(TILES)]
         picked = {}
-        x_rows = {}
+        x_rows = {0: keep.tile([P, PACK, M], BF16, name="x_rows0", align_bytes=64)}
         x_c = [keep.tile([P, M], U32, name="x_c0", align_bytes=64)]
         x_s = [keep.tile([P, M], U8, name=f"x_s{b}", align_bytes=64) for b in range(BLOCKS)]
 
@@ -74,13 +74,13 @@ def tile_list_giclee_gamut_features_kernel(
         nc.gpsimd.memset(w4s_raw[:].bitcast(I32), 0)
 
         nc.sync.dma_start(out=w1_raw[0][:], in_=w1_v[:, :, cols(0)])
-        for q in range(4):
-            nc.sync.dma_start(out=tab_s[32 * q : 32 * q + 4, :].bitcast(I32), in_=tab_scales[0, 4 * q : 4 * q + 4, :].bitcast(I32))
+        for r in range(4):
+            nc.sync.dma_start(out=tab_s[r:P:32, :].bitcast(I32), in_=tab_scales[0, r:16:4, :].bitcast(I32))
         nc.sync.dma_start(offs_t[:], offs)
         nc.sync.dma_start(out=w4_raw[:].bitcast(I32), in_=w4_words[0].bitcast(I32))
         nc.sync.dma_start(out=tab[:].bitcast(I32), in_=tab_words[0].rearrange("p t i -> p (t i)").bitcast(I32))
-        for q in range(4):
-            nc.sync.dma_start(out=w4s_raw[32 * q : 32 * q + 4, :].bitcast(I32), in_=w4_scales[0, 4 * q : 4 * q + 4, :].bitcast(I32))
+        for r in range(4):
+            nc.sync.dma_start(out=w4s_raw[r:P:32, :].bitcast(I32), in_=w4_scales[0, r:16:4, :].bitcast(I32))
         nc.sync.dma_start(out=w1_raw[1][:], in_=w1_v[:, :, cols(1)])
         nc.sync.dma_start(pos_t[:], pos1)
         nc.sync.dma_start(out=w2_raw[0, 0][:], in_=w2_v[0][:, :, cols(0)])
@@ -88,7 +88,7 @@ def tile_list_giclee_gamut_features_kernel(
         nc.sync.dma_start(out=skip_t[:].rearrange("p (b t) -> p b t", t=PACK), in_=skip.rearrange("(b p t) -> p b t", b=BLOCKS, t=PACK))
         nc.sync.dma_start(out=w2_raw[1, 0][:], in_=w2_v[1][:, :, cols(0)])
         wgo_v = wgo.rearrange("(p t) m -> p (t m)", t=PACK)
-        for q in range(4):
+        for q in (0, 2, 1, 3):
             nc.sync.dma_start(out=wgo_t[32 * q : 32 * (q + 1), :], in_=wgo_v)
         for b in range(BLOCKS):
             for t in range(PACK):
@@ -166,6 +166,10 @@ def tile_list_giclee_gamut_features_kernel(
             b, t = divmod(i, PACK)
             picked[i] = keep.tile([P, M], F32, name="picked", tag=f"lead{(i + 1) % TILES}", align_bytes=64)
             nc.vector.tensor_copy(out=picked[i][:], in_=u[i][:].indirect(pos_t[:]))
+            if b == 0:
+                nc.gpsimd.tensor_scalar(
+                    out=x_rows[0][:, t, :], in0=picked[i][:], scalar1=gain_t[:, i : i + 1], scalar2=0.0, op0=ALU.mult, op1=ALU.add
+                )
             engine = nc.vector if i == TILES - 1 else nc.gpsimd
             engine.tensor_tensor(out=weighed[b][:, t, :], in0=picked[i][:], in1=wgo_t[:, t * M : (t + 1) * M], op=ALU.mult)
 
@@ -219,11 +223,8 @@ def tile_list_giclee_gamut_features_kernel(
         pick(6)
         early = row_factors(0, EARLY, "w2_raw10")
         pick(7)
-        x_rows[0] = keep.tile([P, PACK, M], BF16, name="x_rows0", tag="trail_b", align_bytes=64)
         x_rows[1] = keep.tile([P, PACK, M], BF16, name="x_rows1", tag="x_rows1", align_bytes=64)
-        for i in range(PACK):
-            round_picked(i)
-        quantize(x_c[0], x_s[0], weave_picked(0))
+        quantize(x_c[0], x_s[0], weave_picked(0, "trail_b"))
         for i in range(PACK, TILES):
             round_picked(i)
         grouped1 = weave_picked(1, "woven1")

from contextlib import ExitStack

import concourse.mybir as mybir

K, H, T, S, M = 512, 1024, 4096, 1024, 512
FLOPS = 2 * (2 * K * H * S + H * H * M)

F32 = mybir.dt.float32
BF16 = mybir.dt.bfloat16
I32 = mybir.dt.int32
U32 = mybir.dt.uint32
U16 = mybir.dt.uint16
U8 = mybir.dt.uint8
FP8X4 = mybir.dt.float8_e4m3fn_x4
FP4X4 = mybir.dt.float4_e2m1fn_x4
ACT = mybir.ActivationFunctionType
ALU = mybir.AluOpType

P = 128
PACK = 4
PASS = P * PACK
BANK = 512
BLOCKS = H // PASS
TILES = BLOCKS * PACK
HALVES = S // BANK
EARLY = 5


def tile_list_giclee_gamut_features_kernel(
    tc, tab_words, tab_scales, offs, w1, w4_words, w4_scales, gain, pos1, w2, skip, paper, wgo, out
):
    nc = tc.nc
    with ExitStack() as ctx:
        keep = ctx.enter_context(tc.tile_pool(name="keep", bufs=1))
        ring = ctx.enter_context(tc.tile_pool(name="ring", bufs=2))
        psum = ctx.enter_context(tc.psum_pool(name="psum", bufs=4))

        offs_t = keep.tile([P, S // 16], U16, name="offs_t")
        pos_t = keep.tile([P, M // 16], U16, name="pos_t")
        tab = keep.tile([P, T], U32, name="tab")
        tab_s = keep.tile([P, T], U8, name="tab_s")
        w4_raw = keep.tile([P, 2 * H], U8, name="w4_raw")
        w4s_raw = keep.tile([P, H], U8, name="w4s_raw")
        w4_c = keep.tile([P, 2 * H], U8, name="w4_c", align_bytes=64)
        w4_s = [keep.tile([P, P], U8, name=f"w4_s{i}", align_bytes=64) for i in range(TILES)]
        v_c = [keep.tile([P, BANK], U32, name=f"v_c{h}", align_bytes=64) for h in range(HALVES)]
        v_s = keep.tile([P, S], U8, name="v_s", align_bytes=64)
        gain_t = keep.tile([P, TILES], F32, name="gain_t")
        skip_t = keep.tile([P, TILES], F32, name="skip_t")
        half_t = keep.tile([P, TILES], F32, name="half_t")
        wgo_t = keep.tile([P, PACK * M], F32, name="wgo_t")
        w1_raw = [keep.tile([P, PACK, PASS], F32, name=f"w1_raw{b}", tag=f"w1_raw{b}", align_bytes=64) for b in range(BLOCKS)]
        w2_raw = {(a, b): keep.tile([P, PACK, PASS], F32, name=f"w2_raw{a}{b}", tag=f"w2_raw{a}{b}", align_bytes=64) for b in range(BLOCKS) for a in range(BLOCKS)}
        w1_c = [keep.tile([P, PASS], U32, name=f"w1_c{b}", align_bytes=64) for b in range(BLOCKS)]
        w1_s = [keep.tile([P, PASS], U8, name=f"w1_s{b}", align_bytes=64) for b in range(BLOCKS)]
        w2_c = {key: keep.tile([P, PASS], U32, name=f"w2_c{key[0]}{key[1]}", align_bytes=64) for key in w2_raw if key[1] == 0}
        w2_s = {key: keep.tile([P, PASS], U8, name=f"w2_s{key[0]}{key[1]}", align_bytes=64) for key in w2_raw}
        u = [keep.tile([P, S], F32, name=f"u{i}", tag=f"u{i}", align_bytes=64) for i in range(TILES)]
        page = [keep.tile([P, S], F32, name=f"page{i}") for i in range(TILES)]
        picked = {}
        x_rows = {0: keep.tile([P, PACK, M], BF16, name="x_rows0", align_bytes=64)}
        x_c = [keep.tile([P, M], U32, name="x_c0", align_bytes=64)]
        x_s = [keep.tile([P, M], U8, name=f"x_s{b}", align_bytes=64) for b in range(BLOCKS)]

        w1_v = w1.rearrange("(p j) c -> p j c", j=PACK)
        w2_v = w2.rearrange("(a p j) c -> a p j c", a=BLOCKS, j=PACK)
        paper_v = paper.rearrange("(b p t) j -> b t p j", b=BLOCKS, t=PACK)
        out_v = out.rearrange("(b p t) j -> b t p j", b=BLOCKS, t=PACK)

        def cols(b):
            return slice(b * PASS, (b + 1) * PASS)

        nc.vector.memset(tab_s[:].bitcast(I32), 0)
        nc.gpsimd.memset(w4s_raw[:].bitcast(I32), 0)

        nc.sync.dma_start(out=w1_raw[0][:], in_=w1_v[:, :, cols(0)])
        for r in range(4):
            nc.sync.dma_start(out=tab_s[r:P:32, :].bitcast(I32), in_=tab_scales[0, r:16:4, :].bitcast(I32))
        nc.sync.dma_start(offs_t[:], offs)
        nc.sync.dma_start(out=w4_raw[:].bitcast(I32), in_=w4_words[0].bitcast(I32))
        nc.sync.dma_start(out=tab[:].bitcast(I32), in_=tab_words[0].rearrange("p t i -> p (t i)").bitcast(I32))
        for r in range(4):
            nc.sync.dma_start(out=w4s_raw[r:P:32, :].bitcast(I32), in_=w4_scales[0, r:16:4, :].bitcast(I32))
        nc.sync.dma_start(out=w1_raw[1][:], in_=w1_v[:, :, cols(1)])
        nc.sync.dma_start(pos_t[:], pos1)
        nc.sync.dma_start(out=w2_raw[0, 0][:], in_=w2_v[0][:, :, cols(0)])
        nc.sync.dma_start(out=gain_t[:].rearrange("p (b t) -> p b t", t=PACK), in_=gain.rearrange("(b p t) -> p b t", b=BLOCKS, t=PACK))
        nc.sync.dma_start(out=skip_t[:].rearrange("p (b t) -> p b t", t=PACK), in_=skip.rearrange("(b p t) -> p b t", b=BLOCKS, t=PACK))
        nc.sync.dma_start(out=w2_raw[1, 0][:], in_=w2_v[1][:, :, cols(0)])
        wgo_v = wgo.rearrange("(p t) m -> p (t m)", t=PACK)
        for q in (0, 2, 1, 3):
            nc.sync.dma_start(out=wgo_t[32 * q : 32 * (q + 1), :], in_=wgo_v)
        for b in range(BLOCKS):
            for t in range(PACK):
                nc.sync.dma_start(out=page[b * PACK + t][:], in_=paper_v[b, t])
            nc.sync.dma_start(out=w2_raw[b, 1][:], in_=w2_v[b][:, :, cols(1)])

        def new_grouped(tag=None):
            if tag is None:
                return ring.tile([P, PASS * PACK], BF16, name="grouped", align_bytes=64, bufs=3)
            return keep.tile([P, PASS * PACK], BF16, name="grouped", align_bytes=64, tag=tag)

        def round_weight(copy, grouped, raw, m0, m1):
            dst = grouped[:].rearrange("p (t m j) -> p m t j", t=PACK, j=PACK)
            src = raw[:].rearrange("p j (m t) -> p m t j", t=PACK)
            copy(out=dst[:, m0:m1], in_=src[:, m0:m1])

        def weight_steps(codes, scales, raw, tag=None):
            grouped = new_grouped(tag)

            def first():
                round_weight(nc.scalar.copy, grouped, raw, 0, P // 2)

            def second():
                round_weight(nc.scalar.copy, grouped, raw, P // 2, P)
                quantize(codes, scales, grouped)

            return [first, second]

        def quantize(codes, scales, grouped):
            nc.vector.quantize_mx(out=codes[:].bitcast(FP8X4), scales=scales[:], in_=grouped[:])

        nc.vector.tensor_copy(
            out=w4_c[:].bitcast(U16).rearrange("p (b t m) -> p b m t", b=BLOCKS, t=PACK),
            in_=w4_raw[:].bitcast(U16).rearrange("p (b m t) -> p b m t", b=BLOCKS, t=PACK),
        )
        g0 = new_grouped()
        round_weight(nc.vector.tensor_copy, g0, w1_raw[0], 0, P)
        nc.vector.tensor_copy(out=v_s[:], in_=tab_s[:].indirect(offs_t[:]))
        quantize(w1_c[0], w1_s[0], g0)
        w4s_dealt = w4s_raw[:].rearrange("p (b m t) -> p b t m", b=BLOCKS, t=PACK)
        for i in range(TILES):
            nc.gpsimd.tensor_copy(out=w4_s[i][:], in_=w4s_dealt[:, i // PACK, i % PACK, :])
        for h in range(HALVES):
            nc.vector.tensor_copy(out=v_c[h][:], in_=tab[:].indirect(offs_t[:, h * (BANK // 16) : (h + 1) * (BANK // 16)]))

        def first_stage(i, tag):
            b, t = divmod(i, PACK)
            for h in range(HALVES):
                js = slice(h * BANK, (h + 1) * BANK)
                bent = psum.tile([P, BANK], F32, name="bent", bufs=2)
                nc.tensor.matmul_mx(
                    out=bent[:],
                    lhsT=w1_c[b][:, t * P : (t + 1) * P].bitcast(FP8X4),
                    lhsT_scale=w1_s[b][:, t * P : (t + 1) * P],
                    rhs=v_c[h][:].bitcast(FP8X4),
                    rhs_scale=v_s[:, js],
                    start=True,
                    stop=True,
                )
                flat = psum.tile([P, BANK], F32, name="flat", bufs=6)
                nc.tensor.matmul_mx(
                    out=flat[:],
                    lhsT=w4_c[:, 2 * P * i : 2 * P * (i + 1)].bitcast(FP4X4),
                    lhsT_scale=w4_s[i][:],
                    rhs=v_c[h][:].bitcast(FP8X4),
                    rhs_scale=v_s[:, js],
                    start=True,
                    stop=True,
                )
                bent_sb = keep.tile([P, BANK], F32, name="bent_sb", tag=(f"lead{i}", tag)[h], align_bytes=64)
                nc.scalar.activation(out=bent_sb[:], in_=bent[:], func=ACT.Tanh)
                nc.vector.tensor_tensor(out=u[i][:, js], in0=flat[:], in1=bent_sb[:], op=ALU.add)

        def pick(i):
            b, t = divmod(i, PACK)
            picked[i] = keep.tile([P, M], F32, name="picked", tag=f"lead{(i + 1) % TILES}", align_bytes=64)
            nc.vector.tensor_copy(out=picked[i][:], in_=u[i][:].indirect(pos_t[:]))
            if b == 0:
                nc.gpsimd.tensor_scalar(
                    out=x_rows[0][:, t, :], in0=picked[i][:], scalar1=gain_t[:, i : i + 1], scalar2=0.0, op0=ALU.mult, op1=ALU.add
                )
            engine = nc.vector if i == TILES - 1 else nc.gpsimd
            engine.tensor_tensor(out=weighed[b][:, t, :], in0=picked[i][:], in1=wgo_t[:, t * M : (t + 1) * M], op=ALU.mult)

        def round_picked(i):
            b, t = divmod(i, PACK)
            nc.scalar.activation(out=x_rows[b][:, t, :], in_=picked[i][:], func=ACT.Copy, scale=gain_t[:, i : i + 1])

        def weave_picked(b, tag=None):
            grouped = new_grouped(tag)
            nc.scalar.copy(
                out=grouped[:].rearrange("p (c i t) -> p c t i", i=4, t=PACK),
                in_=x_rows[b][:].rearrange("p t (c i) -> p c t i", i=4),
            )
            return grouped

        def row_factors(i0, i1, tag):
            factors = keep.tile([P, i1 - i0], F32, name="factors", tag=tag, align_bytes=64)
            nc.vector.tensor_tensor(out=factors[:], in0=gain_t[:, i0:i1], in1=skip_t[:, i0:i1], op=ALU.mult)
            return factors

        def floor_pages(i0, i1, factors):
            for i in range(i0, i1):
                nc.vector.scalar_tensor_tensor(
                    out=page[i][:], in0=u[i][:], scalar=factors[:, i - i0 : i - i0 + 1], in1=page[i][:], op0=ALU.mult, op1=ALU.max
                )

        weighed = [None, None]
        weighed[0] = keep.tile([P, PACK, M], F32, name="weighed0", tag="w1_raw0", align_bytes=64)

        first_stage(0, "trail_a")
        first_stage(1, "trail_b")
        pick(0)
        first_stage(2, "trail_c")
        pick(1)
        for step in weight_steps(w1_c[1], w1_s[1], w1_raw[1]):
            step()
        first_stage(3, "w1_raw1")
        weighed[1] = keep.tile([P, PACK, M], F32, name="weighed1", tag="w1_raw1", align_bytes=64)
        pick(2)
        first_stage(4, "trail_a")
        pick(3)
        for step in weight_steps(w2_c[0, 0], w2_s[0, 0], w2_raw[0, 0]):
            step()
        first_stage(5, "w2_raw00")
        pick(4)
        first_stage(6, "trail_b")
        pick(5)
        for step in weight_steps(w2_c[1, 0], w2_s[1, 0], w2_raw[1, 0], "x_rows1"):
            step()
        first_stage(7, "w2_raw10")
        pick(6)
        early = row_factors(0, EARLY, "w2_raw10")
        pick(7)
        x_rows[1] = keep.tile([P, PACK, M], BF16, name="x_rows1", tag="x_rows1", align_bytes=64)
        quantize(x_c[0], x_s[0], weave_picked(0, "trail_b"))
        for i in range(PACK, TILES):
            round_picked(i)
        grouped1 = weave_picked(1, "woven1")
        floor_pages(0, EARLY, early)
        x_c.append(keep.tile([P, M], U32, name="x_c1", tag="u3", align_bytes=64))
        quantize(x_c[1], x_s[1], grouped1)
        late = row_factors(EARLY, TILES, "woven1")
        nc.vector.scalar_tensor_tensor(out=half_t[:], in0=gain_t[:], scalar=0.5, in1=skip_t[:], op0=ALU.mult, op1=ALU.mult)
        floor_pages(EARLY, TILES, late)

        def second_stage(i):
            b, t = divmod(i, PACK)
            y = psum.tile([P, BANK], F32, name="flat", bufs=6)
            for a in range(BLOCKS):
                nc.tensor.matmul_mx(
                    out=y[:],
                    lhsT=w2_c[a, b][:, t * P : (t + 1) * P].bitcast(FP8X4),
                    lhsT_scale=w2_s[a, b][:, t * P : (t + 1) * P],
                    rhs=x_c[a][:].bitcast(FP8X4),
                    rhs_scale=x_s[a][:],
                    start=(a == 0),
                    stop=(a == BLOCKS - 1),
                )
            gate = ring.tile([P, M], F32, name="gate", bufs=2)
            nc.scalar.activation(out=gate[:], in_=y[:], func=ACT.Tanh, scale=0.5)
            if i < BLOCKS:
                scaled = keep.tile([P, M], F32, name="scaled", tag=f"u{6 + i}", align_bytes=64)
            elif i == 3:
                scaled = keep.tile([P, M], F32, name="scaled", tag="x_rows1", align_bytes=64)
            else:
                scaled = ring.tile([P, M], F32, name="scaled", bufs=3)
            nc.scalar.activation(out=scaled[:], in_=gate[:], func=ACT.Identity, scale=half_t[:, i : i + 1], bias=half_t[:, i : i + 1])
            nc.vector.tensor_tensor(out=page[i][:].indirect(pos_t[:]), in0=scaled[:], in1=weighed[b][:, t, :], op=ALU.mult)
            nc.sync.dma_start(out=out_v[b, t], in_=page[i][:])

        for i in range(TILES):
            second_stage(i)
            if i < BLOCKS:
                w2_c[i, 1] = keep.tile([P, PASS], U32, name="w2_c", tag=f"u{6 + i}", align_bytes=64)
                for step in weight_steps(w2_c[i, 1], w2_s[i, 1], w2_raw[i, 1], "x_rows1"):
                    step()
